import numpy as np
import ml_dtypes


def mxq(x, axis, fmt="e4m3"):
    dtype, down = {"e4m3": (ml_dtypes.float8_e4m3fn, 7), "e5m2": (ml_dtypes.float8_e5m2, 14)}[fmt]
    v = np.moveaxis(np.asarray(x, np.float32).astype(ml_dtypes.bfloat16).astype(np.float64), axis, -1)
    blocks = v.reshape(v.shape[:-1] + (-1, 32))
    amax = np.abs(blocks).max(-1, keepdims=True)
    byte = np.maximum(np.where(amax > 0, np.frexp(amax)[1] - 1 + 127, 0) - down, 1)
    scale = np.exp2(byte - 127.0)
    codes = (blocks / scale).astype(np.float32).astype(dtype).astype(np.float64)
    return np.moveaxis((codes * scale).reshape(v.shape), -1, axis)


WIDE = False


def mx_kscale(k):
    if not WIDE:
        return np.ones(k)
    levels = np.array([10, -10, 5, -5, 0])
    if k % 512:
        return np.exp2(np.random.permutation(np.resize(levels, k // 32))).repeat(32)
    a = np.empty((k // 512, 16))
    for p in range(k // 512):
        a[p, :8] = np.random.permutation(np.resize(levels, 8))
        for g in range(8):
            far = levels[np.abs(levels - a[p, g]) >= 10]
            a[p, g + 8] = far[np.random.randint(len(far))]
    return np.exp2(a.ravel()).repeat(32)


def f64(x):
    return np.asarray(x).astype(np.float64)


def striped(idx):
    return np.tile(idx.reshape(-1, 16).T, (8, 1)).astype(np.uint16)


def unstriped(offs):
    return offs[:16].T.reshape(-1).astype(np.int64)


def pack_weight(w):
    k, n = w.shape
    w = f64(np.asarray(w, np.float32).astype(ml_dtypes.bfloat16)).reshape(k // 32, 32, n)
    amax = np.abs(w).max(1)
    byte = np.clip(np.where(amax > 0, np.frexp(amax)[1] - 1 + 127 - 7, 1), 1, 254)
    scaled = (w * np.exp2(127.0 - byte)[:, None, :]).reshape(k, n).astype(np.float32)
    words = np.ascontiguousarray(scaled.reshape(k // 512, 128, 4, n).transpose(0, 1, 3, 2)).astype(ml_dtypes.float8_e4m3fn).view(np.uint8)
    return words, np.ascontiguousarray(byte.astype(np.uint8).reshape(k // 512, 16, n))


def unpack_weight(words, scales):
    g, p, n, _ = words.shape
    vals = np.ascontiguousarray(words).view(ml_dtypes.float8_e4m3fn).astype(np.float64) * np.repeat(np.exp2(scales.astype(np.float64) - 127.0), 8, axis=1)[..., None]
    return vals.transpose(0, 1, 3, 2).reshape(g * 512, n)


def relu(v):
    return np.maximum(v, 0.0)


K, T, E, C, N = 1024, 2048, 4, 128, 512


def by_expert(wq, xq):
    return np.concatenate([wq[e].T @ xq[:, e * C:(e + 1) * C] for e in range(E)], axis=1)


def setup_inputs():
    n = np.random.standard_normal
    s = mx_kscale(K)[:, None]
    packed = [pack_weight(m) for m in n((E, K, N)) / np.sqrt(K) / s[None]]
    return {
        "xT": (n((K, T)) * s).astype(np.float32),
        "w_words": np.stack([m[0] for m in packed]),
        "w_scales": np.stack([m[1] for m in packed]),
        "b": (0.3 * n((N, E))).astype(np.float32),
        "gate": np.tile(np.random.uniform(0.2, 1.0, E * C), (N, 1)).astype(np.float32),
        "offs": striped(np.random.permutation(T)[:E * C]),
    }


def reference(xT, w_words, w_scales, b, gate, offs):
    idx = unstriped(offs)
    xq = mxq(f64(xT)[:, idx], 0, "e4m3")
    w = np.stack([unpack_weight(w_words[e], w_scales[e]) for e in range(E)])
    y = by_expert(w, xq)
    y = relu(y + np.repeat(f64(b), C, axis=1))
    out = np.zeros((N, T))
    out[:, idx] = f64(gate) * y
    return out

@@ -1,0 +1,149 @@
+from contextlib import ExitStack
+
+import concourse.mybir as mybir
+
+K, T, E, C, N = 1024, 2048, 4, 128, 512
+FLOPS = 2 * K * N * E * C
+
+F32 = mybir.dt.float32
+BF16 = mybir.dt.bfloat16
+I32 = mybir.dt.int32
+U32 = mybir.dt.uint32
+U16 = mybir.dt.uint16
+U8 = mybir.dt.uint8
+FP8X4 = mybir.dt.float8_e4m3fn_x4
+
+P = 128
+PACK = 4
+PASSES = K // (P * PACK)
+SLOTS = E * C
+HALF = SLOTS // 2
+NBLK = N // P
+
+
+def tile_routed_moe_kernel(tc, xT, w_words, w_scales, b, gate, offs, out):
+    nc = tc.nc
+    relu = mybir.ActivationFunctionType.Relu
+    mult = mybir.AluOpType.mult
+
+    with ExitStack() as ctx:
+        lists = ctx.enter_context(tc.tile_pool(name="lists", bufs=1))
+        keep = ctx.enter_context(tc.tile_pool(name="keep", bufs=1))
+        psum = ctx.enter_context(tc.psum_pool(name="psum", bufs=8))
+
+        offs_sb = lists.tile([P, SLOTS // 16], U16, name="offs_sb")
+        b_sb = keep.tile([P, NBLK, E], F32, name="b_sb")
+
+        warm = keep.tile([P, 2], F32, name="warm")
+        nc.vector.memset(warm[:, 0:1], 0.0)
+        nc.scalar.activation(out=warm[:, 1:2], in_=warm[:, 0:1], func=relu)
+
+        sc = [keep.tile([P, N], U8, name="sc%d" % h, align_bytes=64) for h in range(2)]
+        for h in range(2):
+            nc.vector.memset(sc[h][:].bitcast(I32), 0)
+        win = [keep.tile([P, T], F32, name="win%d" % nb) for nb in range(NBLK)]
+        for nb in range(NBLK):
+            nc.vector.memset(win[nb][:], 0.0)
+
+        x_view = xT.rearrange("(g p t) n -> g t p n", p=P, t=PACK)
+        planes = [keep.tile([P, T], F32, name="plane%d" % i) for i in range(PASSES * PACK)]
+        ws8 = w_scales.rearrange("e a q n -> (e a) q n")
+
+        def load_plane(i):
+            nc.sync.dma_start(out=planes[i][:], in_=x_view[i // PACK, i % PACK])
+
+        def load_scales(h):
+            for q in range(4):
+                nc.gpsimd.dma_start(
+                    out=sc[h][32 * q : 32 * q + 16, :].bitcast(F32),
+                    in_=ws8[4 * h : 4 * h + 4, 4 * q : 4 * q + 4, :].bitcast(F32),
+                )
+
+        load_plane(0)
+        nc.sync.dma_start(offs_sb[:], offs)
+        for i in range(1, 8):
+            load_plane(i)
+        load_scales(0)
+        load_scales(1)
+
+        w_view = w_words.rearrange("e a p n r -> p (e a) (n r)")
+        wt = [[keep.tile([P, 4, P], I32, name="wt%d%d" % (nb, h), align_bytes=64) for h in range(2)] for nb in range(NBLK)]
+        gt = [keep.tile([P, SLOTS], F32, name="gt%d" % nb) for nb in range(NBLK)]
+
+        def load_words(nb, h):
+            nc.sync.dma_start(
+                out=wt[nb][h][:],
+                in_=w_view[:, 4 * h : 4 * h + 4, 4 * P * nb : 4 * P * (nb + 1)].bitcast(I32),
+            )
+
+        def load_gate(nb):
+            nc.sync.dma_start(out=gt[nb][:], in_=gate[P * nb : P * (nb + 1), :])
+
+        load_words(0, 0)
+        nc.sync.dma_start(out=b_sb[:], in_=b.rearrange("(nb p) e -> p nb e", p=P))
+        load_gate(0)
+        load_words(0, 1)
+        for nb in range(1, NBLK):
+            load_words(nb, 0)
+            load_words(nb, 1)
+            load_gate(nb)
+
+        xi = [keep.tile([P, SLOTS, PACK], BF16, name="xi%d" % g, align_bytes=64) for g in range(PASSES)]
+        xc = [keep.tile([P, SLOTS], U32, name="xc%d" % g, align_bytes=64) for g in range(PASSES)]
+        xs = [keep.tile([P, SLOTS], U8, name="xs%d" % g, align_bytes=64) for g in range(PASSES)]
+
+        def gather(g, t, j0, n):
+            nc.vector.tensor_copy(
+                out=xi[g][:, j0 : j0 + n, t],
+                in_=planes[PACK * g + t][:].indirect(offs_sb[:, j0 // 16 : (j0 + n) // 16]),
+            )
+
+        def quantize(g, j0, n):
+            nc.vector.quantize_mx(
+                out=xc[g][:, j0 : j0 + n].bitcast(FP8X4),
+                scales=xs[g][:, j0 : j0 + n],
+                in_=xi[g][:, j0 : j0 + n, :].rearrange("p j t -> p (j t)"),
+            )
+
+        for t in range(PACK):
+            gather(0, t, 0, SLOTS)
+        quantize(0, 0, SLOTS)
+        for t in range(PACK - 1):
+            gather(1, t, 0, SLOTS)
+        for h in range(2):
+            gather(1, PACK - 1, HALF * h, HALF)
+            quantize(1, HALF * h, HALF)
+
+        units = [(0, 0, 2), (0, 2, 2), (1, 0, 4), (2, 0, 4), (3, 0, 4)]
+        for u, (nb, e0, ne) in enumerate(units):
+            ys = keep.tile([P, C * ne], F32, name="ys%d" % u)
+            for i in range(ne):
+                e = e0 + i
+                h = e // 2
+                acc = psum.tile([P, C], F32, name="acc")
+                for a in range(PASSES):
+                    j = 2 * (e % 2) + a
+                    nc.tensor.matmul_mx(
+                        out=acc[:],
+                        lhsT=wt[nb][h][:, j, :].bitcast(FP8X4),
+                        lhsT_scale=sc[h][4 * j : P, P * nb : P * (nb + 1)],
+                        rhs=xc[a][:, C * e : C * (e + 1)].bitcast(FP8X4),
+                        rhs_scale=xs[a][:, C * e : C * (e + 1)],
+                        start=(a == 0),
+                        stop=(a == PASSES - 1),
+                    )
+                nc.scalar.activation(
+                    out=ys[:, C * i : C * (i + 1)],
+                    in_=acc[:],
+                    func=relu,
+                    bias=b_sb[:, nb, e : e + 1],
+                    scale=1.0,
+                )
+            nc.vector.tensor_tensor(
+                out=win[nb][:].indirect(offs_sb[:, (C // 16) * e0 : (C // 16) * (e0 + ne)]),
+                in0=ys[:],
+                in1=gt[nb][:, C * e0 : C * (e0 + ne)],
+                op=mult,
+            )
+            if e0 + ne == E:
+                nc.sync.dma_start(out=out[P * nb : P * (nb + 1), :], in_=win[nb][:])

@@ -32,7 +32,7 @@ def tile_routed_moe_kernel(tc, xT, w_words, w_scales, b, gate, offs, out):
         psum = ctx.enter_context(tc.psum_pool(name="psum", bufs=8))
 
         offs_sb = lists.tile([P, SLOTS // 16], U16, name="offs_sb")
-        b_sb = keep.tile([P, NBLK, E], F32, name="b_sb")
+        b_sb = [keep.tile([P, E], F32, name="b_sb%d" % nb) for nb in range(NBLK)]
 
         warm = keep.tile([P, 2], F32, name="warm")
         nc.vector.memset(warm[:, 0:1], 0.0)
@@ -76,17 +76,22 @@ def tile_routed_moe_kernel(tc, xT, w_words, w_scales, b, gate, offs, out):
                 in_=w_view[:, 4 * h : 4 * h + 4, 4 * P * nb : 4 * P * (nb + 1)].bitcast(I32),
             )
 
-        def load_gate(nb):
-            nc.sync.dma_start(out=gt[nb][:], in_=gate[P * nb : P * (nb + 1), :])
+        def load_gate(nb, j0, n):
+            nc.sync.dma_start(out=gt[nb][:, j0 : j0 + n], in_=gate[P * nb : P * (nb + 1), j0 : j0 + n])
+
+        def load_bias(nb):
+            nc.sync.dma_start(out=b_sb[nb][:], in_=b[P * nb : P * (nb + 1), :])
 
         load_words(0, 0)
-        nc.sync.dma_start(out=b_sb[:], in_=b.rearrange("(nb p) e -> p nb e", p=P))
-        load_gate(0)
+        load_bias(0)
+        load_gate(0, 0, HALF)
         load_words(0, 1)
+        load_gate(0, HALF, HALF)
         for nb in range(1, NBLK):
             load_words(nb, 0)
+            load_bias(nb)
             load_words(nb, 1)
-            load_gate(nb)
+            load_gate(nb, 0, SLOTS)
 
         xi = [keep.tile([P, SLOTS, PACK], BF16, name="xi%d" % g, align_bytes=64) for g in range(PASSES)]
         xc = [keep.tile([P, SLOTS], U32, name="xc%d" % g, align_bytes=64) for g in range(PASSES)]
@@ -136,7 +141,7 @@ def tile_routed_moe_kernel(tc, xT, w_words, w_scales, b, gate, offs, out):
                     out=ys[:, C * i : C * (i + 1)],
                     in_=acc[:],
                     func=relu,
-                    bias=b_sb[:, nb, e : e + 1],
+                    bias=b_sb[nb][:, e : e + 1],
                     scale=1.0,
                 )
             nc.vector.tensor_tensor(

@@ -54,17 +54,15 @@ def tile_routed_moe_kernel(tc, xT, w_words, w_scales, b, gate, offs, out):
 
         def load_scales(h):
             for q in range(4):
-                nc.gpsimd.dma_start(
-                    out=sc[h][32 * q : 32 * q + 16, :].bitcast(F32),
-                    in_=ws8[4 * h : 4 * h + 4, 4 * q : 4 * q + 4, :].bitcast(F32),
+                nc.sync.dma_start(
+                    out=sc[h][32 * q : 32 * q + 16, :].bitcast(I32),
+                    in_=ws8[4 * h : 4 * h + 4, 4 * q : 4 * q + 4, :].bitcast(I32),
                 )
 
         load_plane(0)
         nc.sync.dma_start(offs_sb[:], offs)
         for i in range(1, 8):
             load_plane(i)
-        load_scales(0)
-        load_scales(1)
 
         w_view = w_words.rearrange("e a p n r -> p (e a) (n r)")
         wt = [[keep.tile([P, 4, P], I32, name="wt%d%d" % (nb, h), align_bytes=64) for h in range(2)] for nb in range(NBLK)]
@@ -82,9 +80,11 @@ def tile_routed_moe_kernel(tc, xT, w_words, w_scales, b, gate, offs, out):
         def load_bias(nb):
             nc.sync.dma_start(out=b_sb[nb][:], in_=b[P * nb : P * (nb + 1), :])
 
+        load_scales(0)
         load_words(0, 0)
         load_bias(0)
         load_gate(0, 0, HALF)
+        load_scales(1)
         load_words(0, 1)
         load_gate(0, HALF, HALF)
         for nb in range(1, NBLK):

@@ -84,10 +84,15 @@ def tile_routed_moe_kernel(tc, xT, w_words, w_scales, b, gate, offs, out):
         load_words(0, 0)
         load_bias(0)
         load_gate(0, 0, HALF)
+        load_words(1, 0)
+        load_bias(1)
+        load_gate(1, 0, HALF)
         load_scales(1)
         load_words(0, 1)
         load_gate(0, HALF, HALF)
-        for nb in range(1, NBLK):
+        load_words(1, 1)
+        load_gate(1, HALF, HALF)
+        for nb in range(2, NBLK):
             load_words(nb, 0)
             load_bias(nb)
             load_words(nb, 1)
@@ -119,7 +124,7 @@ def tile_routed_moe_kernel(tc, xT, w_words, w_scales, b, gate, offs, out):
             gather(1, PACK - 1, HALF * h, HALF)
             quantize(1, HALF * h, HALF)
 
-        units = [(0, 0, 2), (0, 2, 2), (1, 0, 4), (2, 0, 4), (3, 0, 4)]
+        units = [(0, 0, 2), (1, 0, 2), (0, 2, 2), (1, 2, 2), (2, 0, 4), (3, 0, 4)]
         for u, (nb, e0, ne) in enumerate(units):
             ys = keep.tile([P, C * ne], F32, name="ys%d" % u)
             for i in range(ne):

@@ -127,14 +127,14 @@ def tile_routed_moe_kernel(tc, xT, w_words, w_scales, b, gate, offs, out):
         units = [(0, 0, 2), (1, 0, 2), (0, 2, 2), (1, 2, 2), (2, 0, 4), (3, 0, 4)]
         for u, (nb, e0, ne) in enumerate(units):
             ys = keep.tile([P, C * ne], F32, name="ys%d" % u)
-            for i in range(ne):
-                e = e0 + i
-                h = e // 2
-                acc = psum.tile([P, C], F32, name="acc")
-                for a in range(PASSES):
+            accs = [psum.tile([P, C], F32, name="acc") for i in range(ne)]
+            for a in range(PASSES):
+                for i in range(ne):
+                    e = e0 + i
+                    h = e // 2
                     j = 2 * (e % 2) + a
                     nc.tensor.matmul_mx(
-                        out=acc[:],
+                        out=accs[i][:],
                         lhsT=wt[nb][h][:, j, :].bitcast(FP8X4),
                         lhsT_scale=sc[h][4 * j : P, P * nb : P * (nb + 1)],
                         rhs=xc[a][:, C * e : C * (e + 1)].bitcast(FP8X4),
@@ -142,9 +142,11 @@ def tile_routed_moe_kernel(tc, xT, w_words, w_scales, b, gate, offs, out):
                         start=(a == 0),
                         stop=(a == PASSES - 1),
                     )
+            for i in range(ne):
+                e = e0 + i
                 nc.scalar.activation(
                     out=ys[:, C * i : C * (i + 1)],
-                    in_=acc[:],
+                    in_=accs[i][:],
                     func=relu,
                     bias=b_sb[nb][:, e : e + 1],
                     scale=1.0,

@@ -120,9 +120,11 @@ def tile_routed_moe_kernel(tc, xT, w_words, w_scales, b, gate, offs, out):
         quantize(0, 0, SLOTS)
         for t in range(PACK - 1):
             gather(1, t, 0, SLOTS)
-        for h in range(2):
-            gather(1, PACK - 1, HALF * h, HALF)
-            quantize(1, HALF * h, HALF)
+        gather(1, PACK - 1, 0, HALF)
+        quantize(1, 0, C)
+        quantize(1, C, C)
+        gather(1, PACK - 1, HALF, HALF)
+        quantize(1, HALF, HALF)
 
         units = [(0, 0, 2), (1, 0, 2), (0, 2, 2), (1, 2, 2), (2, 0, 4), (3, 0, 4)]
         for u, (nb, e0, ne) in enumerate(units):

@@ -87,16 +87,20 @@ def tile_routed_moe_kernel(tc, xT, w_words, w_scales, b, gate, offs, out):
         load_words(1, 0)
         load_bias(1)
         load_gate(1, 0, HALF)
+        load_words(2, 0)
+        load_bias(2)
+        load_gate(2, 0, HALF)
         load_scales(1)
         load_words(0, 1)
         load_gate(0, HALF, HALF)
         load_words(1, 1)
         load_gate(1, HALF, HALF)
-        for nb in range(2, NBLK):
-            load_words(nb, 0)
-            load_bias(nb)
-            load_words(nb, 1)
-            load_gate(nb, 0, SLOTS)
+        load_words(2, 1)
+        load_gate(2, HALF, HALF)
+        load_words(3, 0)
+        load_bias(3)
+        load_words(3, 1)
+        load_gate(3, 0, SLOTS)
 
         xi = [keep.tile([P, SLOTS, PACK], BF16, name="xi%d" % g, align_bytes=64) for g in range(PASSES)]
         xc = [keep.tile([P, SLOTS], U32, name="xc%d" % g, align_bytes=64) for g in range(PASSES)]
@@ -126,7 +130,7 @@ def tile_routed_moe_kernel(tc, xT, w_words, w_scales, b, gate, offs, out):
         gather(1, PACK - 1, HALF, HALF)
         quantize(1, HALF, HALF)
 
-        units = [(0, 0, 2), (1, 0, 2), (0, 2, 2), (1, 2, 2), (2, 0, 4), (3, 0, 4)]
+        units = [(0, 0, 2), (1, 0, 2), (2, 0, 2), (0, 2, 2), (1, 2, 2), (2, 2, 2), (3, 0, 4)]
         for u, (nb, e0, ne) in enumerate(units):
             ys = keep.tile([P, C * ne], F32, name="ys%d" % u)
             accs = [psum.tile([P, C], F32, name="acc") for i in range(ne)]

@@ -127,7 +127,12 @@ def tile_routed_moe_kernel(tc, xT, w_words, w_scales, b, gate, offs, out):
         gather(1, PACK - 1, 0, HALF)
         quantize(1, 0, C)
         quantize(1, C, C)
-        gather(1, PACK - 1, HALF, HALF)
+        late = keep.tile([P, HALF], F32, name="late")
+        nc.vector.tensor_copy(
+            out=late[:],
+            in_=planes[PASSES * PACK - 1][:].indirect(offs_sb[:, HALF // 16 : SLOTS // 16]),
+        )
+        nc.scalar.copy(out=xi[PASSES - 1][:, HALF:SLOTS, PACK - 1], in_=late[:])
         quantize(1, HALF, HALF)
 
         units = [(0, 0, 2), (1, 0, 2), (2, 0, 2), (0, 2, 2), (1, 2, 2), (2, 2, 2), (3, 0, 4)]

@@ -45,12 +45,17 @@ def tile_routed_moe_kernel(tc, xT, w_words, w_scales, b, gate, offs, out):
         for nb in range(NBLK):
             nc.vector.memset(win[nb][:], 0.0)
 
-        x_view = xT.rearrange("(g p t) n -> g t p n", p=P, t=PACK)
-        planes = [keep.tile([P, T], F32, name="plane%d" % i) for i in range(PASSES * PACK)]
+        x_view = xT.rearrange("(g p t) n -> g p t n", p=P, t=PACK)
+        pairs = [keep.tile([P, 2, T], F32, name="pair%d" % i) for i in range(3)]
+        lone = [keep.tile([P, T], F32, name="lone%d" % i) for i in range(2)]
+        planes = [pairs[i // 2][:, i % 2, :] for i in range(6)] + [lone[i][:] for i in range(2)]
         ws8 = w_scales.rearrange("e a q n -> (e a) q n")
 
-        def load_plane(i):
-            nc.sync.dma_start(out=planes[i][:], in_=x_view[i // PACK, i % PACK])
+        def load_pair(i):
+            nc.sync.dma_start(out=pairs[i][:], in_=x_view[i // 2, :, 2 * (i % 2) : 2 * (i % 2) + 2, :])
+
+        def load_lone(i):
+            nc.sync.dma_start(out=lone[i][:], in_=x_view[1, :, 2 + i, :])
 
         def load_scales(h):
             for q in range(4):
@@ -59,10 +64,12 @@ def tile_routed_moe_kernel(tc, xT, w_words, w_scales, b, gate, offs, out):
                     in_=ws8[4 * h : 4 * h + 4, 4 * q : 4 * q + 4, :].bitcast(I32),
                 )
 
-        load_plane(0)
+        load_pair(0)
         nc.sync.dma_start(offs_sb[:], offs)
-        for i in range(1, 8):
-            load_plane(i)
+        load_pair(1)
+        load_pair(2)
+        load_lone(0)
+        load_lone(1)
 
         w_view = w_words.rearrange("e a p n r -> p (e a) (n r)")
         wt = [[keep.tile([P, 4, P], I32, name="wt%d%d" % (nb, h), align_bytes=64) for h in range(2)] for nb in range(NBLK)]
@@ -109,7 +116,7 @@ def tile_routed_moe_kernel(tc, xT, w_words, w_scales, b, gate, offs, out):
         def gather(g, t, j0, n):
             nc.vector.tensor_copy(
                 out=xi[g][:, j0 : j0 + n, t],
-                in_=planes[PACK * g + t][:].indirect(offs_sb[:, j0 // 16 : (j0 + n) // 16]),
+                in_=planes[PACK * g + t].indirect(offs_sb[:, j0 // 16 : (j0 + n) // 16]),
             )
 
         def quantize(g, j0, n):
@@ -122,15 +129,18 @@ def tile_routed_moe_kernel(tc, xT, w_words, w_scales, b, gate, offs, out):
         for t in range(PACK):
             gather(0, t, 0, SLOTS)
         quantize(0, 0, SLOTS)
-        for t in range(PACK - 1):
-            gather(1, t, 0, SLOTS)
+        rows = keep.tile([P, 2, SLOTS], F32, name="rows")
+        for t in range(2):
+            nc.vector.tensor_copy(out=rows[:, t, :], in_=planes[PACK + t].indirect(offs_sb[:]))
+        nc.scalar.copy(out=xi[1][:, :, 0:2], in_=rows[:].rearrange("p t j -> p j t"))
+        gather(1, 2, 0, SLOTS)
         gather(1, PACK - 1, 0, HALF)
         quantize(1, 0, C)
         quantize(1, C, C)
         late = keep.tile([P, HALF], F32, name="late")
         nc.vector.tensor_copy(
             out=late[:],
-            in_=planes[PASSES * PACK - 1][:].indirect(offs_sb[:, HALF // 16 : SLOTS // 16]),
+            in_=planes[PASSES * PACK - 1].indirect(offs_sb[:, HALF // 16 : SLOTS // 16]),
         )
         nc.scalar.copy(out=xi[PASSES - 1][:, HALF:SLOTS, PACK - 1], in_=late[:])
         quantize(1, HALF, HALF)

@@ -94,20 +94,16 @@ def tile_routed_moe_kernel(tc, xT, w_words, w_scales, b, gate, offs, out):
         load_words(1, 0)
         load_bias(1)
         load_gate(1, 0, HALF)
-        load_words(2, 0)
-        load_bias(2)
-        load_gate(2, 0, HALF)
         load_scales(1)
         load_words(0, 1)
         load_gate(0, HALF, HALF)
         load_words(1, 1)
         load_gate(1, HALF, HALF)
-        load_words(2, 1)
-        load_gate(2, HALF, HALF)
-        load_words(3, 0)
-        load_bias(3)
-        load_words(3, 1)
-        load_gate(3, 0, SLOTS)
+        for nb in (2, 3):
+            load_words(nb, 0)
+            load_bias(nb)
+            load_words(nb, 1)
+            load_gate(nb, 0, SLOTS)
 
         xi = [keep.tile([P, SLOTS, PACK], BF16, name="xi%d" % g, align_bytes=64) for g in range(PASSES)]
         xc = [keep.tile([P, SLOTS], U32, name="xc%d" % g, align_bytes=64) for g in range(PASSES)]
@@ -145,7 +141,7 @@ def tile_routed_moe_kernel(tc, xT, w_words, w_scales, b, gate, offs, out):
         nc.scalar.copy(out=xi[PASSES - 1][:, HALF:SLOTS, PACK - 1], in_=late[:])
         quantize(1, HALF, HALF)
 
-        units = [(0, 0, 2), (1, 0, 2), (2, 0, 2), (0, 2, 2), (1, 2, 2), (2, 2, 2), (3, 0, 4)]
+        units = [(0, 0, 2), (1, 0, 2), (0, 2, 2), (1, 2, 2), (2, 0, 4), (3, 0, 4)]
         for u, (nb, e0, ne) in enumerate(units):
             ys = keep.tile([P, C * ne], F32, name="ys%d" % u)
             accs = [psum.tile([P, C], F32, name="acc") for i in range(ne)]

@@ -32,7 +32,8 @@ def tile_routed_moe_kernel(tc, xT, w_words, w_scales, b, gate, offs, out):
         psum = ctx.enter_context(tc.psum_pool(name="psum", bufs=8))
 
         offs_sb = lists.tile([P, SLOTS // 16], U16, name="offs_sb")
-        b_sb = [keep.tile([P, E], F32, name="b_sb%d" % nb) for nb in range(NBLK)]
+        b_first = keep.tile([P, E], F32, name="b_first")
+        b_rest = keep.tile([P, NBLK - 1, E], F32, name="b_rest")
 
         warm = keep.tile([P, 2], F32, name="warm")
         nc.vector.memset(warm[:, 0:1], 0.0)
@@ -72,37 +73,42 @@ def tile_routed_moe_kernel(tc, xT, w_words, w_scales, b, gate, offs, out):
         load_lone(1)
 
         w_view = w_words.rearrange("e a p n r -> p (e a) (n r)")
-        wt = [[keep.tile([P, 4, P], I32, name="wt%d%d" % (nb, h), align_bytes=64) for h in range(2)] for nb in range(NBLK)]
+        wt_a = [keep.tile([P, 4, P], I32, name="wt_a%d" % nb, align_bytes=64) for nb in range(2)]
+        wt_b = keep.tile([P, 4, 2 * P], I32, name="wt_b", align_bytes=64)
+        wt_all = [keep.tile([P, 8, P], I32, name="wt_all%d" % nb, align_bytes=64) for nb in range(2)]
         gt = [keep.tile([P, SLOTS], F32, name="gt%d" % nb) for nb in range(NBLK)]
 
-        def load_words(nb, h):
+        def load_words(tile, pass0, passes, nb, blocks):
             nc.sync.dma_start(
-                out=wt[nb][h][:],
-                in_=w_view[:, 4 * h : 4 * h + 4, 4 * P * nb : 4 * P * (nb + 1)].bitcast(I32),
+                out=tile[:],
+                in_=w_view[:, pass0 : pass0 + passes, 4 * P * nb : 4 * P * (nb + blocks)].bitcast(I32),
             )
+
+        def weights(nb, i):
+            if nb >= 2:
+                return wt_all[nb - 2][:, i, :]
+            if i < 4:
+                return wt_a[nb][:, i, :]
+            return wt_b[:, i - 4, P * nb : P * (nb + 1)]
 
         def load_gate(nb, j0, n):
             nc.sync.dma_start(out=gt[nb][:, j0 : j0 + n], in_=gate[P * nb : P * (nb + 1), j0 : j0 + n])
 
-        def load_bias(nb):
-            nc.sync.dma_start(out=b_sb[nb][:], in_=b[P * nb : P * (nb + 1), :])
+        def bias(nb, e):
+            return b_first[:, e : e + 1] if nb == 0 else b_rest[:, nb - 1, e : e + 1]
 
         load_scales(0)
-        load_words(0, 0)
-        load_bias(0)
+        load_words(wt_a[0], 0, 4, 0, 1)
+        nc.sync.dma_start(out=b_first[:], in_=b[0:P, :])
         load_gate(0, 0, HALF)
-        load_words(1, 0)
-        load_bias(1)
-        load_gate(1, 0, HALF)
+        load_words(wt_a[1], 0, 4, 1, 1)
+        nc.sync.dma_start(out=b_rest[:], in_=b[P:N, :].rearrange("(nb p) e -> p nb e", p=P))
+        load_gate(1, 0, SLOTS)
         load_scales(1)
-        load_words(0, 1)
+        load_words(wt_b, 4, 4, 0, 2)
         load_gate(0, HALF, HALF)
-        load_words(1, 1)
-        load_gate(1, HALF, HALF)
         for nb in (2, 3):
-            load_words(nb, 0)
-            load_bias(nb)
-            load_words(nb, 1)
+            load_words(wt_all[nb - 2], 0, 8, nb, 1)
             load_gate(nb, 0, SLOTS)
 
         xi = [keep.tile([P, SLOTS, PACK], BF16, name="xi%d" % g, align_bytes=64) for g in range(PASSES)]
@@ -152,7 +158,7 @@ def tile_routed_moe_kernel(tc, xT, w_words, w_scales, b, gate, offs, out):
                     j = 2 * (e % 2) + a
                     nc.tensor.matmul_mx(
                         out=accs[i][:],
-                        lhsT=wt[nb][h][:, j, :].bitcast(FP8X4),
+                        lhsT=weights(nb, 2 * e + a).bitcast(FP8X4),
                         lhsT_scale=sc[h][4 * j : P, P * nb : P * (nb + 1)],
                         rhs=xc[a][:, C * e : C * (e + 1)].bitcast(FP8X4),
                         rhs_scale=xs[a][:, C * e : C * (e + 1)],
@@ -165,7 +171,7 @@ def tile_routed_moe_kernel(tc, xT, w_words, w_scales, b, gate, offs, out):
                     out=ys[:, C * i : C * (i + 1)],
                     in_=accs[i][:],
                     func=relu,
-                    bias=b_sb[nb][:, e : e + 1],
+                    bias=bias(nb, e),
                     scale=1.0,
                 )
             nc.vector.tensor_tensor(

@@ -76,7 +76,8 @@ def tile_routed_moe_kernel(tc, xT, w_words, w_scales, b, gate, offs, out):
         wt_a = [keep.tile([P, 4, P], I32, name="wt_a%d" % nb, align_bytes=64) for nb in range(2)]
         wt_b = keep.tile([P, 4, 2 * P], I32, name="wt_b", align_bytes=64)
         wt_all = [keep.tile([P, 8, P], I32, name="wt_all%d" % nb, align_bytes=64) for nb in range(2)]
-        gt = [keep.tile([P, SLOTS], F32, name="gt%d" % nb) for nb in range(NBLK)]
+        gt_two = keep.tile([P, 2, SLOTS], F32, name="gt_two")
+        gt = [gt_two[:, nb, :] for nb in range(2)] + [keep.tile([P, SLOTS], F32, name="gt%d" % nb)[:] for nb in range(2, NBLK)]
 
         def load_words(tile, pass0, passes, nb, blocks):
             nc.sync.dma_start(
@@ -103,10 +104,13 @@ def tile_routed_moe_kernel(tc, xT, w_words, w_scales, b, gate, offs, out):
         load_gate(0, 0, HALF)
         load_words(wt_a[1], 0, 4, 1, 1)
         nc.sync.dma_start(out=b_rest[:], in_=b[P:N, :].rearrange("(nb p) e -> p nb e", p=P))
-        load_gate(1, 0, SLOTS)
+        load_gate(1, 0, HALF)
         load_scales(1)
         load_words(wt_b, 4, 4, 0, 2)
-        load_gate(0, HALF, HALF)
+        nc.sync.dma_start(
+            out=gt_two[:, :, HALF:SLOTS],
+            in_=gate[0 : 2 * P, HALF:SLOTS].rearrange("(nb p) j -> p nb j", p=P),
+        )
         for nb in (2, 3):
             load_words(wt_all[nb - 2], 0, 8, nb, 1)
             load_gate(nb, 0, SLOTS)

from contextlib import ExitStack

import concourse.mybir as mybir

K, T, E, C, N = 1024, 2048, 4, 128, 512
FLOPS = 2 * K * N * E * C

F32 = mybir.dt.float32
BF16 = mybir.dt.bfloat16
I32 = mybir.dt.int32
U32 = mybir.dt.uint32
U16 = mybir.dt.uint16
U8 = mybir.dt.uint8
FP8X4 = mybir.dt.float8_e4m3fn_x4

P = 128
PACK = 4
PASSES = K // (P * PACK)
SLOTS = E * C
HALF = SLOTS // 2
NBLK = N // P


def tile_routed_moe_kernel(tc, xT, w_words, w_scales, b, gate, offs, out):
    nc = tc.nc
    relu = mybir.ActivationFunctionType.Relu
    mult = mybir.AluOpType.mult

    with ExitStack() as ctx:
        lists = ctx.enter_context(tc.tile_pool(name="lists", bufs=1))
        keep = ctx.enter_context(tc.tile_pool(name="keep", bufs=1))
        psum = ctx.enter_context(tc.psum_pool(name="psum", bufs=8))

        offs_sb = lists.tile([P, SLOTS // 16], U16, name="offs_sb")
        b_first = keep.tile([P, E], F32, name="b_first")
        b_rest = keep.tile([P, NBLK - 1, E], F32, name="b_rest")

        warm = keep.tile([P, 2], F32, name="warm")
        nc.vector.memset(warm[:, 0:1], 0.0)
        nc.scalar.activation(out=warm[:, 1:2], in_=warm[:, 0:1], func=relu)

        sc = [keep.tile([P, N], U8, name="sc%d" % h, align_bytes=64) for h in range(2)]
        for h in range(2):
            nc.vector.memset(sc[h][:].bitcast(I32), 0)
        win = [keep.tile([P, T], F32, name="win%d" % nb) for nb in range(NBLK)]
        for nb in range(NBLK):
            nc.vector.memset(win[nb][:], 0.0)

        x_view = xT.rearrange("(g p t) n -> g p t n", p=P, t=PACK)
        pairs = [keep.tile([P, 2, T], F32, name="pair%d" % i) for i in range(3)]
        lone = [keep.tile([P, T], F32, name="lone%d" % i) for i in range(2)]
        planes = [pairs[i // 2][:, i % 2, :] for i in range(6)] + [lone[i][:] for i in range(2)]
        ws8 = w_scales.rearrange("e a q n -> (e a) q n")

        def load_pair(i):
            nc.sync.dma_start(out=pairs[i][:], in_=x_view[i // 2, :, 2 * (i % 2) : 2 * (i % 2) + 2, :])

        def load_lone(i):
            nc.sync.dma_start(out=lone[i][:], in_=x_view[1, :, 2 + i, :])

        def load_scales(h):
            for q in range(4):
                nc.sync.dma_start(
                    out=sc[h][32 * q : 32 * q + 16, :].bitcast(I32),
                    in_=ws8[4 * h : 4 * h + 4, 4 * q : 4 * q + 4, :].bitcast(I32),
                )

        load_pair(0)
        nc.sync.dma_start(offs_sb[:], offs)
        load_pair(1)
        load_pair(2)
        load_lone(0)
        load_lone(1)

        w_view = w_words.rearrange("e a p n r -> p (e a) (n r)")
        wt_a = [keep.tile([P, 4, P], I32, name="wt_a%d" % nb, align_bytes=64) for nb in range(2)]
        wt_b = keep.tile([P, 4, 2 * P], I32, name="wt_b", align_bytes=64)
        wt_all = [keep.tile([P, 8, P], I32, name="wt_all%d" % nb, align_bytes=64) for nb in range(2)]
        gt_two = keep.tile([P, 2, SLOTS], F32, name="gt_two")
        gt = [gt_two[:, nb, :] for nb in range(2)] + [keep.tile([P, SLOTS], F32, name="gt%d" % nb)[:] for nb in range(2, NBLK)]

        def load_words(tile, pass0, passes, nb, blocks):
            nc.sync.dma_start(
                out=tile[:],
                in_=w_view[:, pass0 : pass0 + passes, 4 * P * nb : 4 * P * (nb + blocks)].bitcast(I32),
            )

        def weights(nb, i):
            if nb >= 2:
                return wt_all[nb - 2][:, i, :]
            if i < 4:
                return wt_a[nb][:, i, :]
            return wt_b[:, i - 4, P * nb : P * (nb + 1)]

        def load_gate(nb, j0, n):
            nc.sync.dma_start(out=gt[nb][:, j0 : j0 + n], in_=gate[P * nb : P * (nb + 1), j0 : j0 + n])

        def bias(nb, e):
            return b_first[:, e : e + 1] if nb == 0 else b_rest[:, nb - 1, e : e + 1]

        load_scales(0)
        load_words(wt_a[0], 0, 4, 0, 1)
        nc.sync.dma_start(out=b_first[:], in_=b[0:P, :])
        load_gate(0, 0, HALF)
        load_words(wt_a[1], 0, 4, 1, 1)
        nc.sync.dma_start(out=b_rest[:], in_=b[P:N, :].rearrange("(nb p) e -> p nb e", p=P))
        load_gate(1, 0, HALF)
        load_scales(1)
        load_words(wt_b, 4, 4, 0, 2)
        nc.sync.dma_start(
            out=gt_two[:, :, HALF:SLOTS],
            in_=gate[0 : 2 * P, HALF:SLOTS].rearrange("(nb p) j -> p nb j", p=P),
        )
        for nb in (2, 3):
            load_words(wt_all[nb - 2], 0, 8, nb, 1)
            load_gate(nb, 0, SLOTS)

        xi = [keep.tile([P, SLOTS, PACK], BF16, name="xi%d" % g, align_bytes=64) for g in range(PASSES)]
        xc = [keep.tile([P, SLOTS], U32, name="xc%d" % g, align_bytes=64) for g in range(PASSES)]
        xs = [keep.tile([P, SLOTS], U8, name="xs%d" % g, align_bytes=64) for g in range(PASSES)]

        def gather(g, t, j0, n):
            nc.vector.tensor_copy(
                out=xi[g][:, j0 : j0 + n, t],
                in_=planes[PACK * g + t].indirect(offs_sb[:, j0 // 16 : (j0 + n) // 16]),
            )

        def quantize(g, j0, n):
            nc.vector.quantize_mx(
                out=xc[g][:, j0 : j0 + n].bitcast(FP8X4),
                scales=xs[g][:, j0 : j0 + n],
                in_=xi[g][:, j0 : j0 + n, :].rearrange("p j t -> p (j t)"),
            )

        for t in range(PACK):
            gather(0, t, 0, SLOTS)
        quantize(0, 0, SLOTS)
        rows = keep.tile([P, 2, SLOTS], F32, name="rows")
        for t in range(2):
            nc.vector.tensor_copy(out=rows[:, t, :], in_=planes[PACK + t].indirect(offs_sb[:]))
        nc.scalar.copy(out=xi[1][:, :, 0:2], in_=rows[:].rearrange("p t j -> p j t"))
        gather(1, 2, 0, SLOTS)
        gather(1, PACK - 1, 0, HALF)
        quantize(1, 0, C)
        quantize(1, C, C)
        late = keep.tile([P, HALF], F32, name="late")
        nc.vector.tensor_copy(
            out=late[:],
            in_=planes[PASSES * PACK - 1].indirect(offs_sb[:, HALF // 16 : SLOTS // 16]),
        )
        nc.scalar.copy(out=xi[PASSES - 1][:, HALF:SLOTS, PACK - 1], in_=late[:])
        quantize(1, HALF, HALF)

        units = [(0, 0, 2), (1, 0, 2), (0, 2, 2), (1, 2, 2), (2, 0, 4), (3, 0, 4)]
        for u, (nb, e0, ne) in enumerate(units):
            ys = keep.tile([P, C * ne], F32, name="ys%d" % u)
            accs = [psum.tile([P, C], F32, name="acc") for i in range(ne)]
            for a in range(PASSES):
                for i in range(ne):
                    e = e0 + i
                    h = e // 2
                    j = 2 * (e % 2) + a
                    nc.tensor.matmul_mx(
                        out=accs[i][:],
                        lhsT=weights(nb, 2 * e + a).bitcast(FP8X4),
                        lhsT_scale=sc[h][4 * j : P, P * nb : P * (nb + 1)],
                        rhs=xc[a][:, C * e : C * (e + 1)].bitcast(FP8X4),
                        rhs_scale=xs[a][:, C * e : C * (e + 1)],
                        start=(a == 0),
                        stop=(a == PASSES - 1),
                    )
            for i in range(ne):
                e = e0 + i
                nc.scalar.activation(
                    out=ys[:, C * i : C * (i + 1)],
                    in_=accs[i][:],
                    func=relu,
                    bias=bias(nb, e),
                    scale=1.0,
                )
            nc.vector.tensor_tensor(
                out=win[nb][:].indirect(offs_sb[:, (C // 16) * e0 : (C // 16) * (e0 + ne)]),
                in0=ys[:],
                in1=gt[nb][:, C * e0 : C * (e0 + ne)],
                op=mult,
            )
            if e0 + ne == E:
                nc.sync.dma_start(out=out[P * nb : P * (nb + 1), :], in_=win[nb][:])
